import numpy as np, ml_dtypes
CORES = [1,129,9,137,57,185,105,233,113,241,121,249]
N = 12
KB, QP = 2, 64
MEM = [1,11]
def setup_inputs(rng):
    q = rng.standard_normal((N, 128, QP), dtype=np.float32) / 4; k = rng.standard_normal((N, 128, KB * 128), dtype=np.float32)
    a = 2 * np.pi * rng.random((N, QP)); s = 400 * rng.random((N, QP)) ** 1.5; q[:, 0, :] = s * np.cos(a); q[:, 1, :] = s * np.sin(a); q[:, 2, :] = 150 * rng.standard_normal((N, QP)); k[:, 2, :] = 1 + k[:, 2, :] / 50
    c = np.zeros(N); c[MEM] = rng.permutation(len(MEM))
    a = (2 * np.pi * rng.random() + np.pi / 2 * (c.reshape(N, 1, 1) + 0.5) / len(MEM) - 0.5 + (np.arange(KB).reshape(1, KB, 1) + rng.random((N, KB, 128))) / KB).reshape(N, KB * 128); k[:, 0, :] = np.cos(a); k[:, 1, :] = np.sin(a)
    return {"q": q.astype(ml_dtypes.bfloat16), "k": k.astype(ml_dtypes.bfloat16), "v": rng.standard_normal((N, 128, KB * 128), dtype=np.float32).astype(ml_dtypes.bfloat16)}
def setup_inputs_big(rng):
    d = setup_inputs(rng)
    for k in ("v",): d[k] = (d[k].astype(np.float32) * 1048576.0).astype(d[k].dtype)
    return d
def setup_inputs_small(rng):
    d = setup_inputs(rng)
    for k in ("v",): d[k] = (d[k].astype(np.float32) * (1 / 1048576.0)).astype(d[k].dtype)
    return d
def reference(q, k, v):
    Q, K, V = q.astype(np.float64), k.astype(np.float64), v.astype(np.float64)
    y = np.zeros((N, QP, 128))
    for r in range(N):
        js = list(MEM)
        S = np.concatenate([K[j].T @ Q[r] for j in js], axis=0)
        P = np.exp(S - S.max(axis=0)); P = P / P.sum(axis=0)
        y[r] = P.T @ np.concatenate([V[j][:, 128 * b:128 * b + 128] for j in js for b in range(KB)], axis=0)
    return {"y": y.astype(ml_dtypes.bfloat16)}

@@ -1,0 +1,214 @@
+from concourse.bass import DstId, RemoteDMATransfer
+from concourse.mybir import AluOpType, AxisListType, ActivationFunctionType
+
+QP = 64
+KW = 256
+C_MQ = 128
+C_K = C_MQ + QP
+W_PART = 130
+NE_Q = 8
+NE_F = 8
+NE_Y = 8
+NE_KV = 16
+
+BF, F32 = "bfloat16", "float32"
+SCRATCH = {
+    "kq": ("sbuf", [128, C_K + KW], BF),
+    "vs": ("sbuf", [128, KW], BF),
+    "qb": ("sbuf", [128, 128], BF),
+    "part": ("sbuf", [128, 136], BF),
+    "pland": ("sbuf", [128, 136], BF),
+    "ones": ("sbuf", [128, 128], BF),
+    "ident": ("sbuf", [128, 128], BF),
+    "Pa": ("sbuf", [128, KW], BF), "Pb": ("sbuf", [128, KW], BF),
+    "PTa": ("sbuf", [128, KW], BF), "PTb": ("sbuf", [128, KW], BF),
+    "Dg": ("sbuf", [128, 128], BF),
+    "nmb": ("sbuf", [128, 8], BF),
+    "st": ("sbuf", [128, 16], F32),
+    "yout": ("sbuf", [128, 128], BF),
+    "yland": ("dram", [128, 128], BF),
+    "Sa": ("psum", [128, 512], F32), "Sb": ("psum", [128, 512], F32),
+    "Oa": ("psum", [128, 512], F32), "Ob": ("psum", [128, 512], F32),
+    "T0a": ("psum", [128, 1024], BF), "T1a": ("psum", [128, 1024], BF),
+    "T0b": ("psum", [128, 1024], BF), "T1b": ("psum", [128, 1024], BF),
+}
+SEMAPHORES = (["ld", "ldv", "loc", "yl", "st", "k", "v", "qa", "qbs", "p", "one", "ms", "idn",
+               "OUT", "D", "EE", "DG", "LL", "R", "Y"]
+              + [n + x for x in "ab" for n in ("S", "M", "E0", "E1", "T0", "T1", "C0", "C1", "L")] + ["Oa", "Ob"])
+
+
+def _plan(T, topo):
+    cores = list(T.cores)
+    memc = [cores[r] for r in T.tables["MEM"]]
+    world = range(topo.CORES_PER_HOST * (1 + max(topo.host(c) for c in cores)))
+    sites, tiles = [], []
+    for m in memc:
+        sites.append([c for c in world
+                      if topo.host(c) == topo.host(m) and topo.chip(c) == topo.chip(m) and c not in cores
+                      and all(topo.may_write(c, d) for d in cores)])
+    for j, m in enumerate(memc):
+        grp = [c for c in cores if topo.may_write(c, sites[j][0])]
+        per = len(grp) // len(sites[j])
+        tl = []
+        for t in range(len(sites[j])):
+            ch = grp[t * per:(t + 1) * per]
+            if m in ch:
+                ch = [c for c in ch if c != m] + [m]
+            tl.append(ch)
+        tiles.append(tl)
+    return memc, sites, tiles
+
+
+def _base(tile, m):
+    return C_K - QP * len(tile) if m in tile else 0
+
+
+def _send(g, topo, core, dsts, out_ap, in_ap, rsem, lsem, ne):
+    mask = topo.mask(core, dsts[0])
+    for d in dsts:
+        mask &= topo.mask(core, d)
+    bits = [b for b in range(16) if (mask >> b) & 1][:ne]
+    m = sum(1 << b for b in bits)
+    ids = []
+    for d in dsts:
+        rid, pid = topo.addr(d, core)
+        ids.append(DstId(rid=rid, pnc=pid))
+    g.remote_dma_fused([RemoteDMATransfer(dst_ids=ids, dma_engine_mask=m, remote_sem=rsem,
+                                          srcs=[in_ap], dsts=[out_ap for _ in dsts], alu_op=0)], local_sem=lsem)
+    return len(bits)
+
+
+def _rank(g, core, T, topo, memc, sites, tiles):
+    S = T.sem
+    j = [a for a in range(len(tiles)) if any(core in tl for tl in tiles[a])][0]
+    t = [a for a in range(len(tiles[j])) if core in tiles[j][a]][0]
+    tile = tiles[j][t]
+    i = tile.index(core)
+    qsrc = T.kq[:, C_MQ:C_K]
+    loc = 0
+    if core == memc[j]:
+        g.sync.dma_start(T.kq[:, C_K:C_K + KW], T.k[:, :]).then_inc(S.ld, 16)
+        g.scalar.dma_start(qsrc, T.q[:, :]).then_inc(S.ld, 16)
+        g.sync.dma_start(T.vs[:, :], T.v[:, :]).then_inc(S.ldv, 16)
+        g.wait_ge(S.ld, 32)
+        loc += _send(g, topo, core, sites[j], T.kq[:, C_MQ:C_K + KW], T.kq[:, C_MQ:C_K + KW], S.k, S.loc, NE_KV)
+        g.wait_ge(S.ldv, 16)
+        loc += _send(g, topo, core, sites[j], T.vs[:, :], T.vs[:, :], S.v, S.loc, NE_KV)
+    else:
+        g.sync.dma_start(qsrc, T.q[:, :]).then_inc(S.ld, 16)
+        g.wait_ge(S.ld, 16)
+        col = _base(tile, memc[j]) + QP * i
+        loc += _send(g, topo, core, [sites[j][t]], T.kq[:, col:col + QP], qsrc, S.qa, S.loc, NE_Q)
+    g.sync.wait_ge(S.yl, NE_Y)
+    g.sync.dma_start(T.y[:, :], T.yland[QP * i:QP * i + QP, :]).then_inc(S.st, 16)
+    g.sync.wait_ge(S.st, 16)
+    g.wait_ge(S.loc, loc)
+
+
+def _attend(g, T, X, q_ap, n, q_waits, nm, lout, first):
+    S = T.sem
+    Sp, O, P, PT = T["S" + X], T["O" + X], T["P" + X], T["PT" + X]
+    c0 = 0 if X == "a" else 2
+    for sem, val in q_waits:
+        g.tensor.wait_ge(sem, val)
+    g.tensor.matmul(Sp[:n, 0:KW], q_ap, T.kq[:, C_K:C_K + KW], True, True).then_inc(S["S" + X], 1)
+    g.vector.wait_ge(S["S" + X], 1)
+    g.vector.tensor_reduce(nm, Sp[:n, 0:KW], AxisListType.X, AluOpType.max, negate=True).then_inc(S["M" + X], 1)
+    g.scalar.wait_ge(S["M" + X], 1)
+    for b in range(2):
+        g.scalar.activation(P[:n, 128 * b:128 * b + 128], Sp[:n, 128 * b:128 * b + 128], ActivationFunctionType.Exp,
+                            bias=nm, scale=1.0, accum_out=T.st[:n, c0 + b:c0 + b + 1]).then_inc(S["E%d" % b + X], 1)
+    if first:
+        g.tensor.wait_ge(S.idn, 1)
+    for b in range(2):
+        g.tensor.wait_ge(S["E%d" % b + X], 1)
+        g.tensor.transpose(T["T%d" % b + X][:, 0:n], P[:n, 128 * b:128 * b + 128],
+                           T.ident[:n, :n]).then_inc(S["T%d" % b + X], 1)
+        g.vector.wait_ge(S["T%d" % b + X], 1)
+        g.vector.tensor_copy(PT[:, 128 * b:128 * b + n], T["T%d" % b + X][:, 0:n]).then_inc(S["C%d" % b + X], 1)
+    if first:
+        g.tensor.wait_ge(S.v, NE_KV)
+    for b in range(2):
+        g.tensor.wait_ge(S["C%d" % b + X], 1)
+        mm = g.tensor.matmul(O[:n, 0:128], PT[:, 128 * b:128 * b + n], T.vs[:, 128 * b:128 * b + 128],
+                             b == 0, b == 1 and X == "a")
+        if b == 1 and X == "a":
+            mm.then_inc(S.Oa, 1)
+    g.vector.wait_ge(S["E0" + X], 1)
+    g.vector.wait_ge(S["E1" + X], 1)
+    g.vector.tensor_tensor(lout, T.st[:n, c0:c0 + 1], T.st[:n, c0 + 1:c0 + 2], AluOpType.add).then_inc(S["L" + X], 1)
+
+
+def _site(g, core, T, topo, memc, sites, tiles, j, t):
+    S = T.sem
+    peer = sites[1 - j][t]
+    ta, tb = tiles[j][t], tiles[1 - j][t]
+    na, nb = QP * len(ta), QP * len(tb)
+    base = _base(ta, memc[j])
+    n_direct = len([c for c in ta if c != memc[j]])
+    qa_ap = T.kq[:, base:base + na]
+    loc = 0
+
+    g.vector.memset(T.ones[:, :], 1.0).then_inc(S.one, 1)
+    nms = 0
+    if na < 128:
+        g.vector.memset(T.part[na:128, :], 0.0).then_inc(S.ms, 1)
+        nms += 1
+    if nb < 128:
+        g.vector.memset(T.yout[nb:128, :], 0.0).then_inc(S.ms, 1)
+        nms += 1
+    g.wait_ge(S.one, 1)
+    g.affine_select(T.ident[:, :], T.ones[:, :], [[-1, 128]], AluOpType.is_equal, 0.0, 0, 1).then_inc(S.idn, 1)
+
+    qw = [(S.k, NE_KV)]
+    if n_direct:
+        qw.append((S.qa, NE_Q * n_direct))
+        g.wait_ge(S.qa, NE_Q * n_direct)
+    if n_direct < len(ta):
+        g.wait_ge(S.k, NE_KV)
+    loc += _send(g, topo, core, [peer], T.qb[:, 0:na], qa_ap, S.qbs, S.loc, NE_F)
+    _attend(g, T, "a", qa_ap, na, qw, T.part[:na, 128:129], T.part[:na, 129:130], True)
+    g.vector.wait_ge(S.Oa, 1)
+    g.vector.tensor_copy(T.part[:na, 0:128], T.Oa[:na, 0:128]).then_inc(S.OUT, 1)
+    if nms:
+        g.wait_ge(S.ms, nms)
+    g.wait_ge(S.Ma, 1)
+    g.wait_ge(S.La, 1)
+    g.wait_ge(S.OUT, 1)
+    loc += _send(g, topo, core, [peer], T.pland[:, 0:W_PART], T.part[:, 0:W_PART], S.p, S.loc, NE_F)
+
+    nm = T.nmb[:nb, 0:1]
+    lb, d, e, L, rL = [T.st[:nb, c:c + 1] for c in (4, 5, 6, 7, 8)]
+    _attend(g, T, "b", T.qb[:, 0:nb], nb, [(S.qbs, NE_F)], nm, lb, False)
+    g.vector.wait_ge(S.p, NE_F)
+    g.vector.wait_ge(S.Mb, 1)
+    g.vector.tensor_scalar(d, nm, T.pland[:nb, 128:129], 60.0, AluOpType.subtract, AluOpType.min).then_inc(S.D, 1)
+    g.scalar.wait_ge(S.D, 1)
+    g.scalar.activation(e, d, ActivationFunctionType.Exp).then_inc(S.EE, 1)
+    g.scalar.wait_ge(S.EE, 1)
+    g.scalar.wait_ge(S.idn, 1)
+    g.scalar.activation(T.Dg[:nb, :nb], T.ident[:nb, :nb], ActivationFunctionType.Copy, scale=e).then_inc(S.DG, 1)
+    g.vector.wait_ge(S.EE, 1)
+    g.vector.wait_ge(S.Lb, 1)
+    g.vector.tensor_scalar(L, T.pland[:nb, 129:130], e, lb, AluOpType.mult, AluOpType.add).then_inc(S.LL, 1)
+    g.vector.wait_ge(S.LL, 1)
+    g.vector.reciprocal(rL, L).then_inc(S.R, 1)
+    g.tensor.wait_ge(S.p, NE_F)
+    g.tensor.wait_ge(S.DG, 1)
+    g.tensor.matmul(T.Ob[:nb, 0:128], T.Dg[:nb, :nb], T.pland[:nb, 0:128], False, True).then_inc(S.Ob, 1)
+    g.vector.wait_ge(S.R, 1)
+    g.vector.wait_ge(S.Ob, 1)
+    g.vector.tensor_scalar(T.yout[:nb, :], T.Ob[:nb, 0:128], rL, None, AluOpType.mult).then_inc(S.Y, 1)
+    g.wait_ge(S.Y, 1)
+    loc += _send(g, topo, core, tb, T.yland[:, :], T.yout[:, :], S.yl, S.loc, NE_Y)
+    g.wait_ge(S.loc, loc)
+
+
+def rank_program(g, core, T, topo):
+    memc, sites, tiles = _plan(T, topo)
+    if T.rank_of(core) is not None:
+        _rank(g, core, T, topo, memc, sites, tiles)
+        return
+    for j in range(len(sites)):
+        if core in sites[j]:
+            _site(g, core, T, topo, memc, sites, tiles, j, sites[j].index(core))

@@ -5,7 +5,6 @@ QP = 64
 KW = 256
 C_MQ = 128
 C_K = C_MQ + QP
-W_PART = 130
 NE_Q = 8
 NE_F = 8
 NE_Y = 8
@@ -15,9 +14,9 @@ BF, F32 = "bfloat16", "float32"
 SCRATCH = {
     "kq": ("sbuf", [128, C_K + KW], BF),
     "vs": ("sbuf", [128, KW], BF),
-    "qb": ("sbuf", [128, 128], BF),
+    "kf": ("sbuf", [128, KW], BF),
+    "vf": ("sbuf", [128, KW], BF),
     "part": ("sbuf", [128, 136], BF),
-    "pland": ("sbuf", [128, 136], BF),
     "ones": ("sbuf", [128, 128], BF),
     "ident": ("sbuf", [128, 128], BF),
     "Pa": ("sbuf", [128, KW], BF), "Pb": ("sbuf", [128, KW], BF),
@@ -32,7 +31,7 @@ SCRATCH = {
     "T0a": ("psum", [128, 1024], BF), "T1a": ("psum", [128, 1024], BF),
     "T0b": ("psum", [128, 1024], BF), "T1b": ("psum", [128, 1024], BF),
 }
-SEMAPHORES = (["ld", "ldv", "loc", "yl", "st", "k", "v", "qa", "qbs", "p", "one", "ms", "idn",
+SEMAPHORES = (["ld", "ldv", "loc", "yl", "st", "k", "v", "qa", "kfs", "vfs", "one", "ms", "idn",
                "OUT", "D", "EE", "DG", "LL", "R", "Y"]
               + [n + x for x in "ab" for n in ("S", "M", "E0", "E1", "T0", "T1", "C0", "C1", "L")] + ["Oa", "Ob"])
 
@@ -105,32 +104,40 @@ def _rank(g, core, T, topo, memc, sites, tiles):
     g.wait_ge(S.loc, loc)
 
 
-def _attend(g, T, X, q_ap, n, q_waits, nm, lout, first):
+def _front(g, T, X, q_ap, k_ap, n, waits, nm):
     S = T.sem
-    Sp, O, P, PT = T["S" + X], T["O" + X], T["P" + X], T["PT" + X]
+    Sp, P = T["S" + X], T["P" + X]
     c0 = 0 if X == "a" else 2
-    for sem, val in q_waits:
+    for sem, val in waits:
         g.tensor.wait_ge(sem, val)
-    g.tensor.matmul(Sp[:n, 0:KW], q_ap, T.kq[:, C_K:C_K + KW], True, True).then_inc(S["S" + X], 1)
+    g.tensor.matmul(Sp[:n, 0:KW], q_ap, k_ap, True, True).then_inc(S["S" + X], 1)
     g.vector.wait_ge(S["S" + X], 1)
     g.vector.tensor_reduce(nm, Sp[:n, 0:KW], AxisListType.X, AluOpType.max, negate=True).then_inc(S["M" + X], 1)
     g.scalar.wait_ge(S["M" + X], 1)
     for b in range(2):
         g.scalar.activation(P[:n, 128 * b:128 * b + 128], Sp[:n, 128 * b:128 * b + 128], ActivationFunctionType.Exp,
                             bias=nm, scale=1.0, accum_out=T.st[:n, c0 + b:c0 + b + 1]).then_inc(S["E%d" % b + X], 1)
-    if first:
-        g.tensor.wait_ge(S.idn, 1)
+
+
+def _mid(g, T, X, n):
+    S = T.sem
+    P, PT = T["P" + X], T["PT" + X]
     for b in range(2):
         g.tensor.wait_ge(S["E%d" % b + X], 1)
         g.tensor.transpose(T["T%d" % b + X][:, 0:n], P[:n, 128 * b:128 * b + 128],
                            T.ident[:n, :n]).then_inc(S["T%d" % b + X], 1)
         g.vector.wait_ge(S["T%d" % b + X], 1)
         g.vector.tensor_copy(PT[:, 128 * b:128 * b + n], T["T%d" % b + X][:, 0:n]).then_inc(S["C%d" % b + X], 1)
-    if first:
-        g.tensor.wait_ge(S.v, NE_KV)
+
+
+def _back(g, T, X, v, n, vwait, lout):
+    S = T.sem
+    O, PT = T["O" + X], T["PT" + X]
+    c0 = 0 if X == "a" else 2
+    g.tensor.wait_ge(vwait[0], vwait[1])
     for b in range(2):
         g.tensor.wait_ge(S["C%d" % b + X], 1)
-        mm = g.tensor.matmul(O[:n, 0:128], PT[:, 128 * b:128 * b + n], T.vs[:, 128 * b:128 * b + 128],
+        mm = g.tensor.matmul(O[:n, 0:128], PT[:, 128 * b:128 * b + n], v[:, 128 * b:128 * b + 128],
                              b == 0, b == 1 and X == "a")
         if b == 1 and X == "a":
             mm.then_inc(S.Oa, 1)
@@ -142,65 +149,64 @@ def _attend(g, T, X, q_ap, n, q_waits, nm, lout, first):
 def _site(g, core, T, topo, memc, sites, tiles, j, t):
     S = T.sem
     peer = sites[1 - j][t]
-    ta, tb = tiles[j][t], tiles[1 - j][t]
-    na, nb = QP * len(ta), QP * len(tb)
-    base = _base(ta, memc[j])
-    n_direct = len([c for c in ta if c != memc[j]])
-    qa_ap = T.kq[:, base:base + na]
+    tile = tiles[j][t]
+    n = QP * len(tile)
+    base = _base(tile, memc[j])
+    n_direct = len([c for c in tile if c != memc[j]])
+    q_ap = T.kq[:, base:base + n]
+    k_ap = T.kq[:, C_K:C_K + KW]
     loc = 0
 
     g.vector.memset(T.ones[:, :], 1.0).then_inc(S.one, 1)
-    nms = 0
-    if na < 128:
-        g.vector.memset(T.part[na:128, :], 0.0).then_inc(S.ms, 1)
-        nms += 1
-    if nb < 128:
-        g.vector.memset(T.yout[nb:128, :], 0.0).then_inc(S.ms, 1)
-        nms += 1
+    if n < 128:
+        g.vector.memset(T.yout[n:128, :], 0.0).then_inc(S.ms, 1)
     g.wait_ge(S.one, 1)
     g.affine_select(T.ident[:, :], T.ones[:, :], [[-1, 128]], AluOpType.is_equal, 0.0, 0, 1).then_inc(S.idn, 1)
 
-    qw = [(S.k, NE_KV)]
-    if n_direct:
-        qw.append((S.qa, NE_Q * n_direct))
-        g.wait_ge(S.qa, NE_Q * n_direct)
-    if n_direct < len(ta):
-        g.wait_ge(S.k, NE_KV)
-    loc += _send(g, topo, core, [peer], T.qb[:, 0:na], qa_ap, S.qbs, S.loc, NE_F)
-    _attend(g, T, "a", qa_ap, na, qw, T.part[:na, 128:129], T.part[:na, 129:130], True)
-    g.vector.wait_ge(S.Oa, 1)
-    g.vector.tensor_copy(T.part[:na, 0:128], T.Oa[:na, 0:128]).then_inc(S.OUT, 1)
-    if nms:
-        g.wait_ge(S.ms, nms)
-    g.wait_ge(S.Ma, 1)
-    g.wait_ge(S.La, 1)
-    g.wait_ge(S.OUT, 1)
-    loc += _send(g, topo, core, [peer], T.pland[:, 0:W_PART], T.part[:, 0:W_PART], S.p, S.loc, NE_F)
+    g.wait_ge(S.k, NE_KV)
+    loc += _send(g, topo, core, [peer], T.kf[:, :], k_ap, S.kfs, S.loc, NE_F)
+    g.wait_ge(S.v, NE_KV)
+    loc += _send(g, topo, core, [peer], T.vf[:, :], T.vs[:, :], S.vfs, S.loc, NE_F)
 
-    nm = T.nmb[:nb, 0:1]
-    lb, d, e, L, rL = [T.st[:nb, c:c + 1] for c in (4, 5, 6, 7, 8)]
-    _attend(g, T, "b", T.qb[:, 0:nb], nb, [(S.qbs, NE_F)], nm, lb, False)
-    g.vector.wait_ge(S.p, NE_F)
+    nma, la = T.part[:n, 128:129], T.part[:n, 129:130]
+    nmb = T.nmb[:n, 0:1]
+    lb, d, e, L, rL = [T.st[:n, c:c + 1] for c in (4, 5, 6, 7, 8)]
+    qw = [(S.k, NE_KV)] + ([(S.qa, NE_Q * n_direct)] if n_direct else [])
+
+    _front(g, T, "a", q_ap, k_ap, n, qw, nma)
+    g.tensor.wait_ge(S.idn, 1)
+    _mid(g, T, "a", n)
+    _front(g, T, "b", q_ap, T.kf[:, :], n, [(S.kfs, NE_F)], nmb)
+    _back(g, T, "a", T.vs, n, (S.v, NE_KV), la)
+    g.vector.wait_ge(S.Oa, 1)
+    g.vector.tensor_copy(T.part[:n, 0:128], T.Oa[:n, 0:128]).then_inc(S.OUT, 1)
+    g.vector.wait_ge(S.Ma, 1)
     g.vector.wait_ge(S.Mb, 1)
-    g.vector.tensor_scalar(d, nm, T.pland[:nb, 128:129], 60.0, AluOpType.subtract, AluOpType.min).then_inc(S.D, 1)
+    g.vector.tensor_scalar(d, nmb, nma, 60.0, AluOpType.subtract, AluOpType.min).then_inc(S.D, 1)
+    _mid(g, T, "b", n)
+    _back(g, T, "b", T.vf, n, (S.vfs, NE_F), lb)
+
     g.scalar.wait_ge(S.D, 1)
     g.scalar.activation(e, d, ActivationFunctionType.Exp).then_inc(S.EE, 1)
     g.scalar.wait_ge(S.EE, 1)
     g.scalar.wait_ge(S.idn, 1)
-    g.scalar.activation(T.Dg[:nb, :nb], T.ident[:nb, :nb], ActivationFunctionType.Copy, scale=e).then_inc(S.DG, 1)
+    g.scalar.activation(T.Dg[:n, :n], T.ident[:n, :n], ActivationFunctionType.Copy, scale=e).then_inc(S.DG, 1)
     g.vector.wait_ge(S.EE, 1)
+    g.vector.wait_ge(S.La, 1)
     g.vector.wait_ge(S.Lb, 1)
-    g.vector.tensor_scalar(L, T.pland[:nb, 129:130], e, lb, AluOpType.mult, AluOpType.add).then_inc(S.LL, 1)
+    g.vector.tensor_scalar(L, la, e, lb, AluOpType.mult, AluOpType.add).then_inc(S.LL, 1)
     g.vector.wait_ge(S.LL, 1)
     g.vector.reciprocal(rL, L).then_inc(S.R, 1)
-    g.tensor.wait_ge(S.p, NE_F)
+    g.tensor.wait_ge(S.OUT, 1)
     g.tensor.wait_ge(S.DG, 1)
-    g.tensor.matmul(T.Ob[:nb, 0:128], T.Dg[:nb, :nb], T.pland[:nb, 0:128], False, True).then_inc(S.Ob, 1)
+    g.tensor.matmul(T.Ob[:n, 0:128], T.Dg[:n, :n], T.part[:n, 0:128], False, True).then_inc(S.Ob, 1)
     g.vector.wait_ge(S.R, 1)
     g.vector.wait_ge(S.Ob, 1)
-    g.vector.tensor_scalar(T.yout[:nb, :], T.Ob[:nb, 0:128], rL, None, AluOpType.mult).then_inc(S.Y, 1)
+    g.vector.tensor_scalar(T.yout[:n, :], T.Ob[:n, 0:128], rL, None, AluOpType.mult).then_inc(S.Y, 1)
+    if n < 128:
+        g.wait_ge(S.ms, 1)
     g.wait_ge(S.Y, 1)
-    loc += _send(g, topo, core, tb, T.yland[:, :], T.yout[:, :], S.yl, S.loc, NE_Y)
+    loc += _send(g, topo, core, tile, T.yland[:, :], T.yout[:, :], S.yl, S.loc, NE_Y)
     g.wait_ge(S.loc, loc)
 
 

from concourse.bass import DstId, RemoteDMATransfer
from concourse.mybir import AluOpType, AxisListType, ActivationFunctionType

QP = 64
KW = 256
C_MQ = 128
C_K = C_MQ + QP
NE_Q = 8
NE_F = 8
NE_Y = 8
NE_KV = 16

BF, F32 = "bfloat16", "float32"
SCRATCH = {
    "kq": ("sbuf", [128, C_K + KW], BF),
    "vs": ("sbuf", [128, KW], BF),
    "kf": ("sbuf", [128, KW], BF),
    "vf": ("sbuf", [128, KW], BF),
    "part": ("sbuf", [128, 136], BF),
    "ones": ("sbuf", [128, 128], BF),
    "ident": ("sbuf", [128, 128], BF),
    "Pa": ("sbuf", [128, KW], BF), "Pb": ("sbuf", [128, KW], BF),
    "PTa": ("sbuf", [128, KW], BF), "PTb": ("sbuf", [128, KW], BF),
    "Dg": ("sbuf", [128, 128], BF),
    "nmb": ("sbuf", [128, 8], BF),
    "st": ("sbuf", [128, 16], F32),
    "yout": ("sbuf", [128, 128], BF),
    "yland": ("dram", [128, 128], BF),
    "Sa": ("psum", [128, 512], F32), "Sb": ("psum", [128, 512], F32),
    "Oa": ("psum", [128, 512], F32), "Ob": ("psum", [128, 512], F32),
    "T0a": ("psum", [128, 1024], BF), "T1a": ("psum", [128, 1024], BF),
    "T0b": ("psum", [128, 1024], BF), "T1b": ("psum", [128, 1024], BF),
}
SEMAPHORES = (["ld", "ldv", "loc", "yl", "st", "k", "v", "qa", "kfs", "vfs", "one", "ms", "idn",
               "OUT", "D", "EE", "DG", "LL", "R", "Y"]
              + [n + x for x in "ab" for n in ("S", "M", "E0", "E1", "T0", "T1", "C0", "C1", "L")] + ["Oa", "Ob"])


def _plan(T, topo):
    cores = list(T.cores)
    memc = [cores[r] for r in T.tables["MEM"]]
    world = range(topo.CORES_PER_HOST * (1 + max(topo.host(c) for c in cores)))
    sites, tiles = [], []
    for m in memc:
        sites.append([c for c in world
                      if topo.host(c) == topo.host(m) and topo.chip(c) == topo.chip(m) and c not in cores
                      and all(topo.may_write(c, d) for d in cores)])
    for j, m in enumerate(memc):
        grp = [c for c in cores if topo.may_write(c, sites[j][0])]
        per = len(grp) // len(sites[j])
        tl = []
        for t in range(len(sites[j])):
            ch = grp[t * per:(t + 1) * per]
            if m in ch:
                ch = [c for c in ch if c != m] + [m]
            tl.append(ch)
        tiles.append(tl)
    return memc, sites, tiles


def _base(tile, m):
    return C_K - QP * len(tile) if m in tile else 0


def _send(g, topo, core, dsts, out_ap, in_ap, rsem, lsem, ne):
    mask = topo.mask(core, dsts[0])
    for d in dsts:
        mask &= topo.mask(core, d)
    bits = [b for b in range(16) if (mask >> b) & 1][:ne]
    m = sum(1 << b for b in bits)
    ids = []
    for d in dsts:
        rid, pid = topo.addr(d, core)
        ids.append(DstId(rid=rid, pnc=pid))
    g.remote_dma_fused([RemoteDMATransfer(dst_ids=ids, dma_engine_mask=m, remote_sem=rsem,
                                          srcs=[in_ap], dsts=[out_ap for _ in dsts], alu_op=0)], local_sem=lsem)
    return len(bits)


def _rank(g, core, T, topo, memc, sites, tiles):
    S = T.sem
    j = [a for a in range(len(tiles)) if any(core in tl for tl in tiles[a])][0]
    t = [a for a in range(len(tiles[j])) if core in tiles[j][a]][0]
    tile = tiles[j][t]
    i = tile.index(core)
    qsrc = T.kq[:, C_MQ:C_K]
    loc = 0
    if core == memc[j]:
        g.sync.dma_start(T.kq[:, C_K:C_K + KW], T.k[:, :]).then_inc(S.ld, 16)
        g.scalar.dma_start(qsrc, T.q[:, :]).then_inc(S.ld, 16)
        g.sync.dma_start(T.vs[:, :], T.v[:, :]).then_inc(S.ldv, 16)
        g.wait_ge(S.ld, 32)
        loc += _send(g, topo, core, sites[j], T.kq[:, C_MQ:C_K + KW], T.kq[:, C_MQ:C_K + KW], S.k, S.loc, NE_KV)
        g.wait_ge(S.ldv, 16)
        loc += _send(g, topo, core, sites[j], T.vs[:, :], T.vs[:, :], S.v, S.loc, NE_KV)
    else:
        g.sync.dma_start(qsrc, T.q[:, :]).then_inc(S.ld, 16)
        g.wait_ge(S.ld, 16)
        col = _base(tile, memc[j]) + QP * i
        loc += _send(g, topo, core, [sites[j][t]], T.kq[:, col:col + QP], qsrc, S.qa, S.loc, NE_Q)
    g.sync.wait_ge(S.yl, NE_Y)
    g.sync.dma_start(T.y[:, :], T.yland[QP * i:QP * i + QP, :]).then_inc(S.st, 16)
    g.sync.wait_ge(S.st, 16)
    g.wait_ge(S.loc, loc)


def _front(g, T, X, q_ap, k_ap, n, waits, nm):
    S = T.sem
    Sp, P = T["S" + X], T["P" + X]
    c0 = 0 if X == "a" else 2
    for sem, val in waits:
        g.tensor.wait_ge(sem, val)
    g.tensor.matmul(Sp[:n, 0:KW], q_ap, k_ap, True, True).then_inc(S["S" + X], 1)
    g.vector.wait_ge(S["S" + X], 1)
    g.vector.tensor_reduce(nm, Sp[:n, 0:KW], AxisListType.X, AluOpType.max, negate=True).then_inc(S["M" + X], 1)
    g.scalar.wait_ge(S["M" + X], 1)
    for b in range(2):
        g.scalar.activation(P[:n, 128 * b:128 * b + 128], Sp[:n, 128 * b:128 * b + 128], ActivationFunctionType.Exp,
                            bias=nm, scale=1.0, accum_out=T.st[:n, c0 + b:c0 + b + 1]).then_inc(S["E%d" % b + X], 1)


def _mid(g, T, X, n):
    S = T.sem
    P, PT = T["P" + X], T["PT" + X]
    for b in range(2):
        g.tensor.wait_ge(S["E%d" % b + X], 1)
        g.tensor.transpose(T["T%d" % b + X][:, 0:n], P[:n, 128 * b:128 * b + 128],
                           T.ident[:n, :n]).then_inc(S["T%d" % b + X], 1)
        g.vector.wait_ge(S["T%d" % b + X], 1)
        g.vector.tensor_copy(PT[:, 128 * b:128 * b + n], T["T%d" % b + X][:, 0:n]).then_inc(S["C%d" % b + X], 1)


def _back(g, T, X, v, n, vwait, lout):
    S = T.sem
    O, PT = T["O" + X], T["PT" + X]
    c0 = 0 if X == "a" else 2
    g.tensor.wait_ge(vwait[0], vwait[1])
    for b in range(2):
        g.tensor.wait_ge(S["C%d" % b + X], 1)
        mm = g.tensor.matmul(O[:n, 0:128], PT[:, 128 * b:128 * b + n], v[:, 128 * b:128 * b + 128],
                             b == 0, b == 1 and X == "a")
        if b == 1 and X == "a":
            mm.then_inc(S.Oa, 1)
    g.vector.wait_ge(S["E0" + X], 1)
    g.vector.wait_ge(S["E1" + X], 1)
    g.vector.tensor_tensor(lout, T.st[:n, c0:c0 + 1], T.st[:n, c0 + 1:c0 + 2], AluOpType.add).then_inc(S["L" + X], 1)


def _site(g, core, T, topo, memc, sites, tiles, j, t):
    S = T.sem
    peer = sites[1 - j][t]
    tile = tiles[j][t]
    n = QP * len(tile)
    base = _base(tile, memc[j])
    n_direct = len([c for c in tile if c != memc[j]])
    q_ap = T.kq[:, base:base + n]
    k_ap = T.kq[:, C_K:C_K + KW]
    loc = 0

    g.vector.memset(T.ones[:, :], 1.0).then_inc(S.one, 1)
    if n < 128:
        g.vector.memset(T.yout[n:128, :], 0.0).then_inc(S.ms, 1)
    g.wait_ge(S.one, 1)
    g.affine_select(T.ident[:, :], T.ones[:, :], [[-1, 128]], AluOpType.is_equal, 0.0, 0, 1).then_inc(S.idn, 1)

    g.wait_ge(S.k, NE_KV)
    loc += _send(g, topo, core, [peer], T.kf[:, :], k_ap, S.kfs, S.loc, NE_F)
    g.wait_ge(S.v, NE_KV)
    loc += _send(g, topo, core, [peer], T.vf[:, :], T.vs[:, :], S.vfs, S.loc, NE_F)

    nma, la = T.part[:n, 128:129], T.part[:n, 129:130]
    nmb = T.nmb[:n, 0:1]
    lb, d, e, L, rL = [T.st[:n, c:c + 1] for c in (4, 5, 6, 7, 8)]
    qw = [(S.k, NE_KV)] + ([(S.qa, NE_Q * n_direct)] if n_direct else [])

    _front(g, T, "a", q_ap, k_ap, n, qw, nma)
    g.tensor.wait_ge(S.idn, 1)
    _mid(g, T, "a", n)
    _front(g, T, "b", q_ap, T.kf[:, :], n, [(S.kfs, NE_F)], nmb)
    _back(g, T, "a", T.vs, n, (S.v, NE_KV), la)
    g.vector.wait_ge(S.Oa, 1)
    g.vector.tensor_copy(T.part[:n, 0:128], T.Oa[:n, 0:128]).then_inc(S.OUT, 1)
    g.vector.wait_ge(S.Ma, 1)
    g.vector.wait_ge(S.Mb, 1)
    g.vector.tensor_scalar(d, nmb, nma, 60.0, AluOpType.subtract, AluOpType.min).then_inc(S.D, 1)
    _mid(g, T, "b", n)
    _back(g, T, "b", T.vf, n, (S.vfs, NE_F), lb)

    g.scalar.wait_ge(S.D, 1)
    g.scalar.activation(e, d, ActivationFunctionType.Exp).then_inc(S.EE, 1)
    g.scalar.wait_ge(S.EE, 1)
    g.scalar.wait_ge(S.idn, 1)
    g.scalar.activation(T.Dg[:n, :n], T.ident[:n, :n], ActivationFunctionType.Copy, scale=e).then_inc(S.DG, 1)
    g.vector.wait_ge(S.EE, 1)
    g.vector.wait_ge(S.La, 1)
    g.vector.wait_ge(S.Lb, 1)
    g.vector.tensor_scalar(L, la, e, lb, AluOpType.mult, AluOpType.add).then_inc(S.LL, 1)
    g.vector.wait_ge(S.LL, 1)
    g.vector.reciprocal(rL, L).then_inc(S.R, 1)
    g.tensor.wait_ge(S.OUT, 1)
    g.tensor.wait_ge(S.DG, 1)
    g.tensor.matmul(T.Ob[:n, 0:128], T.Dg[:n, :n], T.part[:n, 0:128], False, True).then_inc(S.Ob, 1)
    g.vector.wait_ge(S.R, 1)
    g.vector.wait_ge(S.Ob, 1)
    g.vector.tensor_scalar(T.yout[:n, :], T.Ob[:n, 0:128], rL, None, AluOpType.mult).then_inc(S.Y, 1)
    if n < 128:
        g.wait_ge(S.ms, 1)
    g.wait_ge(S.Y, 1)
    loc += _send(g, topo, core, tile, T.yland[:, :], T.yout[:, :], S.yl, S.loc, NE_Y)
    g.wait_ge(S.loc, loc)


def rank_program(g, core, T, topo):
    memc, sites, tiles = _plan(T, topo)
    if T.rank_of(core) is not None:
        _rank(g, core, T, topo, memc, sites, tiles)
        return
    for j in range(len(sites)):
        if core in sites[j]:
            _site(g, core, T, topo, memc, sites, tiles, j, sites[j].index(core))
